import numpy as np
import ml_dtypes


def mxq(x, axis, fmt="e4m3"):
    dtype, down = {"e4m3": (ml_dtypes.float8_e4m3fn, 7), "e5m2": (ml_dtypes.float8_e5m2, 14)}[fmt]
    v = np.moveaxis(np.asarray(x, np.float32).astype(ml_dtypes.bfloat16).astype(np.float64), axis, -1)
    blocks = v.reshape(v.shape[:-1] + (-1, 32))
    amax = np.abs(blocks).max(-1, keepdims=True)
    byte = np.maximum(np.where(amax > 0, np.frexp(amax)[1] - 1 + 127, 0) - down, 1)
    scale = np.exp2(byte - 127.0)
    codes = (blocks / scale).astype(np.float32).astype(dtype).astype(np.float64)
    return np.moveaxis((codes * scale).reshape(v.shape), -1, axis)


WIDE = False


def mx_kscale(k):
    if not WIDE:
        return np.ones(k)
    levels = np.array([10, -10, 5, -5, 0])
    if k % 512:
        return np.exp2(np.random.permutation(np.resize(levels, k // 32))).repeat(32)
    a = np.empty((k // 512, 16))
    for p in range(k // 512):
        a[p, :8] = np.random.permutation(np.resize(levels, 8))
        for g in range(8):
            far = levels[np.abs(levels - a[p, g]) >= 10]
            a[p, g + 8] = far[np.random.randint(len(far))]
    return np.exp2(a.ravel()).repeat(32)


def f64(x):
    return np.asarray(x).astype(np.float64)


def striped(idx):
    return np.tile(idx.reshape(-1, 16).T, (8, 1)).astype(np.uint16)


def unstriped(offs):
    return offs[:16].T.reshape(-1).astype(np.int64)


def silu(v):
    return v / (1.0 + np.exp(-np.maximum(v, -700.0)))


K, T, D, S, V, N = 512, 2048, 4, 1024, 512, 128


def setup_inputs():
    n = np.random.standard_normal
    s = mx_kscale(K)[:, None]
    return {
        "xT": (n((K, T)) * s).astype(np.float32),
        "w": (n((K, N)) / np.sqrt(K) / s).astype(np.float32),
        "b": (0.3 * n((N, 1))).astype(np.float32),
        "gate": np.tile(np.random.uniform(0.2, 1.0, (D, 1, V)) / np.sqrt(D), (1, N, 1)).astype(np.float32),
        "offs": striped(np.random.permutation(T)[:S]),
        "pos1": striped(np.random.permutation(S)[:V]),
        "pos2": striped(np.random.permutation(S)[:V]),
        "pos3": striped(np.random.permutation(S)[:V]),
        "pos4": striped(np.random.permutation(S)[:V]),
    }


def reference(xT, w, b, gate, offs, pos1, pos2, pos3, pos4):
    idx = unstriped(offs)
    xq = mxq(f64(xT)[:, idx], 0, "e4m3")
    y = mxq(f64(w), 0, "e4m3").T @ xq
    y = silu(y + f64(b))
    return sum(f64(gate[d]) * y[:, unstriped(p)] for d, p in enumerate((pos1, pos2, pos3, pos4)))

@@ -1,0 +1,153 @@
+from contextlib import ExitStack
+
+import concourse.mybir as mybir
+
+K, T, D, S, V, N = 512, 2048, 4, 1024, 512, 128
+P = 128
+FLOPS = 2 * K * N * S
+
+F32 = mybir.dt.float32
+BF16 = mybir.dt.bfloat16
+U32 = mybir.dt.uint32
+U16 = mybir.dt.uint16
+U8 = mybir.dt.uint8
+FP8X4 = mybir.dt.float8_e4m3fn_x4
+COPY = mybir.ActivationFunctionType.Copy
+SILU = mybir.ActivationFunctionType.Silu
+MULT = mybir.AluOpType.mult
+
+NV = 512
+K2_CHUNKS = ((0, 1024, 0), (1024, 1024, 0))
+PAIR_CHUNKS = ((0, 1024, 768), (1024, 512, 384), (1536, 256, 176), (1792, 256, 160))
+K3_CHUNKS = ((0, 1024, 0), (1024, 512, 0), (1536, 256, 0), (1792, 256, 0))
+K3_GATHERS = (256, 256)
+PIECES = (256, 256, 256, 128, 128)
+
+
+def tile_picked_sub_lin_silu_sub_e_kernel(
+    tc, xT, w, b, gate, offs, pos1, pos2, pos3, pos4, out
+):
+    nc = tc.nc
+    with ExitStack() as ctx:
+        keep = ctx.enter_context(tc.tile_pool(name="keep", bufs=1))
+        turns = ctx.enter_context(tc.tile_pool(name="turns", bufs=1))
+        psum = ctx.enter_context(tc.psum_pool(name="psum", bufs=1))
+
+        warm = keep.tile([P, 1], F32, name="warm")
+        warmed = keep.tile([P, 1], F32, name="warmed")
+        nc.gpsimd.memset(warm[:], 0.0)
+        nc.scalar.activation(warmed[:], warm[:], SILU)
+
+        x_rows = xT.rearrange("(p j) t -> p j t", j=4)
+        offs_t = keep.tile([P, S // 16], U16, name="offs_t")
+        single2 = keep.tile([P, T], F32, name="single2", align_bytes=64)
+        single3 = keep.tile([P, T], F32, name="single3", align_bytes=64)
+        raws = []
+        for i, (t0, n, nv) in enumerate(K2_CHUNKS):
+            nc.sync.dma_start(single2[:, t0 : t0 + n], x_rows[:, 2, t0 : t0 + n])
+            if i == 0:
+                nc.sync.dma_start(offs_t[:], offs)
+        for i, (t0, n, nv) in enumerate(PAIR_CHUNKS):
+            raw = keep.tile([P, 2, n], F32, name=f"raw{i}")
+            nc.sync.dma_start(raw[:], x_rows[:, 0:2, t0 : t0 + n])
+            raws.append(raw)
+        for t0, n, nv in K3_CHUNKS:
+            nc.sync.dma_start(single3[:, t0 : t0 + n], x_rows[:, 3, t0 : t0 + n])
+        w_raw = keep.tile([P, 4, N], F32, name="w_raw")
+        nc.sync.dma_start(w_raw[:], w.rearrange("(p j) n -> p j n", j=4))
+        b_t = keep.tile([P, 1], F32, name="b_t")
+        nc.sync.dma_start(b_t[:], b)
+        gate_t = keep.tile([P, D, V], F32, name="gate_t")
+        nc.sync.dma_start(gate_t[:], gate.rearrange("d p v -> p d v"))
+        pos_ts = []
+        for d, pos in enumerate((pos1, pos2, pos3, pos4)):
+            pos_t = keep.tile([P, V // 16], U16, name=f"pos_t{d}")
+            nc.sync.dma_start(pos_t[:], pos)
+            pos_ts.append(pos_t)
+
+        pair = keep.tile([P, T, 2], BF16, name="pair", align_bytes=64)
+        rounded2 = keep.tile([P, T], BF16, name="rounded2", align_bytes=64)
+        rounded3 = turns.tile([P, T], BF16, name="rounded3", tag="late", align_bytes=64)
+        picked = keep.tile([P, S * 4], BF16, name="picked", align_bytes=64)
+        values = picked[:].rearrange("p (s j) -> p s j", j=4)
+        words = picked[:].bitcast(U32).rearrange("p (s u) -> p s u", u=2)
+        pair_window = pair[:].rearrange("p t e -> p (t e)").bitcast(U32)
+
+        def round_split(dst, src, t0, n, nv):
+            if nv > 0:
+                nc.vector.tensor_copy(dst[:, t0 : t0 + nv], src[:, 0:nv])
+            if nv < n:
+                nc.scalar.activation(dst[:, t0 + nv : t0 + n], src[:, nv:n], COPY)
+
+        def entries(s0, s1):
+            return offs_t[:, s0 // 16 : s1 // 16]
+
+        for t0, n, nv in K2_CHUNKS:
+            round_split(rounded2, single2[:, t0 : t0 + n], t0, n, nv)
+        nc.vector.tensor_copy(values[:, 0:NV, 2], single2[:].indirect(entries(0, NV)))
+        nc.scalar.activation(values[:, NV:S, 2], rounded2[:].indirect(entries(NV, S)), COPY)
+        for raw, (t0, n, nv) in zip(raws, PAIR_CHUNKS):
+            round_split(pair, raw[:].rearrange("p e t -> p t e"), t0, n, nv)
+        nc.vector.tensor_copy(words[:, :, 0], pair_window.indirect(offs_t[:]))
+        for t0, n, nv in K3_CHUNKS:
+            round_split(rounded3, single3[:, t0 : t0 + n], t0, n, nv)
+        s0 = 0
+        for n in K3_GATHERS:
+            nc.vector.tensor_copy(values[:, s0 : s0 + n, 3], single3[:].indirect(entries(s0, s0 + n)))
+            s0 += n
+        nc.scalar.activation(values[:, NV:S, 3], rounded3[:].indirect(entries(NV, S)), COPY)
+
+        w_pack = keep.tile([P, N, 4], BF16, name="w_pack", align_bytes=64)
+        nc.vector.tensor_copy(w_pack[:], w_raw[:].rearrange("p j n -> p n j"))
+        w_codes = keep.tile([P, N], U32, name="w_codes", align_bytes=64)
+        w_scales = keep.tile([P, N], U8, name="w_scales", align_bytes=64)
+        x_codes = keep.tile([P, S], U32, name="x_codes", align_bytes=64)
+        x_scales = keep.tile([P, S], U8, name="x_scales", align_bytes=64)
+        y = turns.tile([P, S], F32, name="y", tag="late", align_bytes=64)
+
+        s0 = 0
+        for i, n in enumerate(PIECES):
+            cols = slice(s0, s0 + n)
+            nc.vector.quantize_mx(
+                out=x_codes[:, cols].bitcast(FP8X4),
+                scales=x_scales[:, cols],
+                in_=picked[:, 4 * s0 : 4 * (s0 + n)],
+            )
+            if i == 0:
+                nc.vector.quantize_mx(
+                    out=w_codes[:].bitcast(FP8X4),
+                    scales=w_scales[:],
+                    in_=w_pack[:].rearrange("p n j -> p (n j)"),
+                )
+            acc = psum.tile([P, n], F32, name=f"acc{s0}")
+            nc.tensor.matmul_mx(
+                out=acc[:],
+                lhsT=w_codes[:].bitcast(FP8X4),
+                lhsT_scale=w_scales[:],
+                rhs=x_codes[:, cols].bitcast(FP8X4),
+                rhs_scale=x_scales[:, cols],
+                start=True,
+                stop=True,
+            )
+            nc.scalar.activation(y[:, cols], acc[:], SILU, bias=b_t[:])
+            s0 += n
+
+        terms = [keep.tile([P, V], F32, name=f"term{d}") for d in range(D)]
+        sum01 = keep.tile([P, V], F32, name="sum01")
+        sum012 = keep.tile([P, V], F32, name="sum012")
+        total = keep.tile([P, V], F32, name="total")
+
+        def neighbour(d):
+            nc.vector.tensor_tensor(terms[d][:], y[:].indirect(pos_ts[d][:]), gate_t[:, d, :], MULT)
+
+        neighbour(0)
+        neighbour(1)
+        neighbour(2)
+        nc.vector.tensor_add(sum01[:], terms[0][:], terms[1][:])
+        neighbour(3)
+        halves = (slice(0, V // 2), slice(V // 2, V))
+        for h in halves:
+            nc.vector.tensor_add(sum012[:, h], sum01[:, h], terms[2][:, h])
+        for h in halves:
+            nc.vector.tensor_add(total[:, h], sum012[:, h], terms[3][:, h])
+            nc.sync.dma_start(out[:, h], total[:, h])

@@ -1,6 +1,7 @@
 from contextlib import ExitStack
 
 import concourse.mybir as mybir
+from concourse.masks import make_identity
 
 K, T, D, S, V, N = 512, 2048, 4, 1024, 512, 128
 P = 128
@@ -37,6 +38,9 @@ def tile_picked_sub_lin_silu_sub_e_kernel(
         warmed = keep.tile([P, 1], F32, name="warmed")
         nc.gpsimd.memset(warm[:], 0.0)
         nc.scalar.activation(warmed[:], warm[:], SILU)
+
+        ident = keep.tile([P, P], F32, name="ident")
+        make_identity(nc, ident[:])
 
         x_rows = xT.rearrange("(p j) t -> p j t", j=4)
         offs_t = keep.tile([P, S // 16], U16, name="offs_t")
@@ -119,7 +123,7 @@ def tile_picked_sub_lin_silu_sub_e_kernel(
                     scales=w_scales[:],
                     in_=w_pack[:].rearrange("p n j -> p (n j)"),
                 )
-            acc = psum.tile([P, n], F32, name=f"acc{s0}")
+            acc = psum.tile([P, n], F32, name=f"acc{s0}", tag=f"bank{i}")
             nc.tensor.matmul_mx(
                 out=acc[:],
                 lhsT=w_codes[:].bitcast(FP8X4),
@@ -133,21 +137,23 @@ def tile_picked_sub_lin_silu_sub_e_kernel(
             s0 += n
 
         terms = [keep.tile([P, V], F32, name=f"term{d}") for d in range(D)]
-        sum01 = keep.tile([P, V], F32, name="sum01")
-        sum012 = keep.tile([P, V], F32, name="sum012")
         total = keep.tile([P, V], F32, name="total")
-
-        def neighbour(d):
+        blocks = [slice(c * P, (c + 1) * P) for c in range(V // P)]
+        turned = [psum.tile([P, P], F32, name=f"turned{c}", tag=f"bank{4 + c}") for c in range(V // P)]
+        for d in range(D):
             nc.vector.tensor_tensor(terms[d][:], y[:].indirect(pos_ts[d][:]), gate_t[:, d, :], MULT)
-
-        neighbour(0)
-        neighbour(1)
-        neighbour(2)
-        nc.vector.tensor_add(sum01[:], terms[0][:], terms[1][:])
-        neighbour(3)
-        halves = (slice(0, V // 2), slice(V // 2, V))
-        for h in halves:
-            nc.vector.tensor_add(sum012[:, h], sum01[:, h], terms[2][:, h])
-        for h in halves:
-            nc.vector.tensor_add(total[:, h], sum012[:, h], terms[3][:, h])
-            nc.sync.dma_start(out[:, h], total[:, h])
+            if d < D - 1:
+                for c, cols in enumerate(blocks):
+                    nc.tensor.matmul(
+                        turned[c][:], terms[d][:, cols], ident[:], start=(d == 0), stop=(d == D - 2), is_transpose=True
+                    )
+        for h in range(2):
+            half = slice(h * V // 2, (h + 1) * V // 2)
+            back = psum.tile([P, V // 2], F32, name=f"back{h}", tag=f"bank{h}")
+            for i in range(2):
+                c = 2 * h + i
+                sum_t = keep.tile([P, P], F32, name=f"sum_t{c}")
+                nc.scalar.copy(sum_t[:], turned[c][:])
+                nc.tensor.transpose(back[:, i * P : (i + 1) * P], sum_t[:], ident[:])
+            nc.vector.tensor_add(total[:, half], back[:], terms[D - 1][:, half])
+            nc.sync.dma_start(out[:, half], total[:, half])

@@ -17,11 +17,11 @@ COPY = mybir.ActivationFunctionType.Copy
 SILU = mybir.ActivationFunctionType.Silu
 MULT = mybir.AluOpType.mult
 
-NV = 512
-K2_CHUNKS = ((0, 1024, 0), (1024, 1024, 0))
-PAIR_CHUNKS = ((0, 1024, 768), (1024, 512, 384), (1536, 256, 176), (1792, 256, 160))
-K3_CHUNKS = ((0, 1024, 0), (1024, 512, 0), (1536, 256, 0), (1792, 256, 0))
-K3_GATHERS = (256, 256)
+NV = 256
+K2_CHUNKS = ((0, 1024, 0), (1024, 1024, 640))
+PAIR_CHUNKS = ((0, 1024, 1024), (1024, 512, 512), (1536, 256, 176), (1792, 256, 160))
+K3_CHUNKS = ((0, 512, 0), (512, 512, 0), (1024, 512, 0), (1536, 256, 0), (1792, 256, 0))
+K3_GATHERS = (256,)
 PIECES = (256, 256, 256, 128, 128)
 
 
@@ -99,7 +99,8 @@ def tile_picked_sub_lin_silu_sub_e_kernel(
         for n in K3_GATHERS:
             nc.vector.tensor_copy(values[:, s0 : s0 + n, 3], single3[:].indirect(entries(s0, s0 + n)))
             s0 += n
-        nc.scalar.activation(values[:, NV:S, 3], rounded3[:].indirect(entries(NV, S)), COPY)
+        for s0 in range(NV, S, 256):
+            nc.scalar.activation(values[:, s0 : s0 + 256, 3], rounded3[:].indirect(entries(s0, s0 + 256)), COPY)
 
         w_pack = keep.tile([P, N, 4], BF16, name="w_pack", align_bytes=64)
         nc.vector.tensor_copy(w_pack[:], w_raw[:].rearrange("p j n -> p n j"))
@@ -138,22 +139,38 @@ def tile_picked_sub_lin_silu_sub_e_kernel(
 
         terms = [keep.tile([P, V], F32, name=f"term{d}") for d in range(D)]
         total = keep.tile([P, V], F32, name="total")
-        blocks = [slice(c * P, (c + 1) * P) for c in range(V // P)]
         turned = [psum.tile([P, P], F32, name=f"turned{c}", tag=f"bank{4 + c}") for c in range(V // P)]
-        for d in range(D):
-            nc.vector.tensor_tensor(terms[d][:], y[:].indirect(pos_ts[d][:]), gate_t[:, d, :], MULT)
+
+        def neighbour(d, v0, v1):
+            nc.vector.tensor_tensor(
+                terms[d][:, v0:v1], y[:].indirect(pos_ts[d][:, v0 // 16 : v1 // 16]), gate_t[:, d, v0:v1], MULT
+            )
             if d < D - 1:
-                for c, cols in enumerate(blocks):
+                for c in range(v0 // P, v1 // P):
                     nc.tensor.matmul(
-                        turned[c][:], terms[d][:, cols], ident[:], start=(d == 0), stop=(d == D - 2), is_transpose=True
+                        turned[c][:],
+                        terms[d][:, c * P : (c + 1) * P],
+                        ident[:],
+                        start=(d == 0),
+                        stop=(d == D - 2),
+                        is_transpose=True,
                     )
+
+        neighbour(0, 0, V)
+        neighbour(1, 0, V)
+        backs = []
         for h in range(2):
-            half = slice(h * V // 2, (h + 1) * V // 2)
+            neighbour(2, h * V // 2, (h + 1) * V // 2)
             back = psum.tile([P, V // 2], F32, name=f"back{h}", tag=f"bank{h}")
             for i in range(2):
                 c = 2 * h + i
                 sum_t = keep.tile([P, P], F32, name=f"sum_t{c}")
                 nc.scalar.copy(sum_t[:], turned[c][:])
                 nc.tensor.transpose(back[:, i * P : (i + 1) * P], sum_t[:], ident[:])
-            nc.vector.tensor_add(total[:, half], back[:], terms[D - 1][:, half])
+            backs.append(back)
+        for h in range(2):
+            neighbour(3, h * V // 2, (h + 1) * V // 2)
+        for h in range(2):
+            half = slice(h * V // 2, (h + 1) * V // 2)
+            nc.vector.tensor_add(total[:, half], backs[h][:], terms[D - 1][:, half])
             nc.sync.dma_start(out[:, half], total[:, half])

@@ -17,12 +17,11 @@ COPY = mybir.ActivationFunctionType.Copy
 SILU = mybir.ActivationFunctionType.Silu
 MULT = mybir.AluOpType.mult
 
-NV = 256
-K2_CHUNKS = ((0, 1024, 0), (1024, 1024, 640))
-PAIR_CHUNKS = ((0, 1024, 1024), (1024, 512, 512), (1536, 256, 176), (1792, 256, 160))
-K3_CHUNKS = ((0, 512, 0), (512, 512, 0), (1024, 512, 0), (1536, 256, 0), (1792, 256, 0))
-K3_GATHERS = (256,)
-PIECES = (256, 256, 256, 128, 128)
+NV = 320
+CHUNKS = (1024, 512, 512)
+LAST_CHUNKS = (1024, 512, 256, 256)
+LAST_GATHERS = (352, 352)
+PIECES = (256, 256, 128, 256, 128)
 
 
 def tile_picked_sub_lin_silu_sub_e_kernel(
@@ -44,19 +43,16 @@ def tile_picked_sub_lin_silu_sub_e_kernel(
 
         x_rows = xT.rearrange("(p j) t -> p j t", j=4)
         offs_t = keep.tile([P, S // 16], U16, name="offs_t")
-        single2 = keep.tile([P, T], F32, name="single2", align_bytes=64)
-        single3 = keep.tile([P, T], F32, name="single3", align_bytes=64)
-        raws = []
-        for i, (t0, n, nv) in enumerate(K2_CHUNKS):
-            nc.sync.dma_start(single2[:, t0 : t0 + n], x_rows[:, 2, t0 : t0 + n])
-            if i == 0:
-                nc.sync.dma_start(offs_t[:], offs)
-        for i, (t0, n, nv) in enumerate(PAIR_CHUNKS):
-            raw = keep.tile([P, 2, n], F32, name=f"raw{i}")
-            nc.sync.dma_start(raw[:], x_rows[:, 0:2, t0 : t0 + n])
-            raws.append(raw)
-        for t0, n, nv in K3_CHUNKS:
-            nc.sync.dma_start(single3[:, t0 : t0 + n], x_rows[:, 3, t0 : t0 + n])
+        planes = []
+        for j in range(4):
+            plane = keep.tile([P, T], F32, name=f"plane{j}", align_bytes=64)
+            t0 = 0
+            for n in CHUNKS if j < 3 else LAST_CHUNKS:
+                nc.sync.dma_start(plane[:, t0 : t0 + n], x_rows[:, j, t0 : t0 + n])
+                if j == 0 and t0 == 0:
+                    nc.sync.dma_start(offs_t[:], offs)
+                t0 += n
+            planes.append(plane)
         w_raw = keep.tile([P, 4, N], F32, name="w_raw")
         nc.sync.dma_start(w_raw[:], w.rearrange("(p j) n -> p j n", j=4))
         b_t = keep.tile([P, 1], F32, name="b_t")
@@ -69,38 +65,26 @@ def tile_picked_sub_lin_silu_sub_e_kernel(
             nc.sync.dma_start(pos_t[:], pos)
             pos_ts.append(pos_t)
 
-        pair = keep.tile([P, T, 2], BF16, name="pair", align_bytes=64)
-        rounded2 = keep.tile([P, T], BF16, name="rounded2", align_bytes=64)
-        rounded3 = turns.tile([P, T], BF16, name="rounded3", tag="late", align_bytes=64)
         picked = keep.tile([P, S * 4], BF16, name="picked", align_bytes=64)
         values = picked[:].rearrange("p (s j) -> p s j", j=4)
-        words = picked[:].bitcast(U32).rearrange("p (s u) -> p s u", u=2)
-        pair_window = pair[:].rearrange("p t e -> p (t e)").bitcast(U32)
-
-        def round_split(dst, src, t0, n, nv):
-            if nv > 0:
-                nc.vector.tensor_copy(dst[:, t0 : t0 + nv], src[:, 0:nv])
-            if nv < n:
-                nc.scalar.activation(dst[:, t0 + nv : t0 + n], src[:, nv:n], COPY)
 
         def entries(s0, s1):
             return offs_t[:, s0 // 16 : s1 // 16]
 
-        for t0, n, nv in K2_CHUNKS:
-            round_split(rounded2, single2[:, t0 : t0 + n], t0, n, nv)
-        nc.vector.tensor_copy(values[:, 0:NV, 2], single2[:].indirect(entries(0, NV)))
-        nc.scalar.activation(values[:, NV:S, 2], rounded2[:].indirect(entries(NV, S)), COPY)
-        for raw, (t0, n, nv) in zip(raws, PAIR_CHUNKS):
-            round_split(pair, raw[:].rearrange("p e t -> p t e"), t0, n, nv)
-        nc.vector.tensor_copy(words[:, :, 0], pair_window.indirect(offs_t[:]))
-        for t0, n, nv in K3_CHUNKS:
-            round_split(rounded3, single3[:, t0 : t0 + n], t0, n, nv)
-        s0 = 0
-        for n in K3_GATHERS:
-            nc.vector.tensor_copy(values[:, s0 : s0 + n, 3], single3[:].indirect(entries(s0, s0 + n)))
-            s0 += n
-        for s0 in range(NV, S, 256):
-            nc.scalar.activation(values[:, s0 : s0 + 256, 3], rounded3[:].indirect(entries(s0, s0 + 256)), COPY)
+        for j, plane in enumerate(planes):
+            if j < 3:
+                rounded = keep.tile([P, T], BF16, name=f"rounded{j}", align_bytes=64)
+            else:
+                rounded = turns.tile([P, T], BF16, name=f"rounded{j}", tag="late", align_bytes=64)
+            t0 = 0
+            for n in CHUNKS if j < 3 else LAST_CHUNKS:
+                nc.vector.tensor_copy(rounded[:, t0 : t0 + n], plane[:, t0 : t0 + n])
+                t0 += n
+            nc.vector.tensor_copy(values[:, 0:NV, j], plane[:].indirect(entries(0, NV)))
+            s0 = NV
+            for n in (S - NV,) if j < 3 else LAST_GATHERS:
+                nc.scalar.activation(values[:, s0 : s0 + n, j], rounded[:].indirect(entries(s0, s0 + n)), COPY)
+                s0 += n
 
         w_pack = keep.tile([P, N, 4], BF16, name="w_pack", align_bytes=64)
         nc.vector.tensor_copy(w_pack[:], w_raw[:].rearrange("p j n -> p n j"))

@@ -16,12 +16,12 @@ FP8X4 = mybir.dt.float8_e4m3fn_x4
 COPY = mybir.ActivationFunctionType.Copy
 SILU = mybir.ActivationFunctionType.Silu
 MULT = mybir.AluOpType.mult
+ADD = mybir.AluOpType.add
 
-NV = 320
 CHUNKS = (1024, 512, 512)
 LAST_CHUNKS = (1024, 512, 256, 256)
-LAST_GATHERS = (352, 352)
-PIECES = (256, 256, 128, 256, 128)
+SHARES = (384, 384, 256)
+PIECES = ((256, 128), (256, 128), (256,))
 
 
 def tile_picked_sub_lin_silu_sub_e_kernel(
@@ -65,8 +65,7 @@ def tile_picked_sub_lin_silu_sub_e_kernel(
             nc.sync.dma_start(pos_t[:], pos)
             pos_ts.append(pos_t)
 
-        picked = keep.tile([P, S * 4], BF16, name="picked", align_bytes=64)
-        values = picked[:].rearrange("p (s j) -> p s j", j=4)
+        picked = [keep.tile([P, n, 4], BF16, name=f"picked{g}", align_bytes=64) for g, n in enumerate(SHARES)]
 
         def entries(s0, s1):
             return offs_t[:, s0 // 16 : s1 // 16]
@@ -80,46 +79,50 @@ def tile_picked_sub_lin_silu_sub_e_kernel(
             for n in CHUNKS if j < 3 else LAST_CHUNKS:
                 nc.vector.tensor_copy(rounded[:, t0 : t0 + n], plane[:, t0 : t0 + n])
                 t0 += n
-            nc.vector.tensor_copy(values[:, 0:NV, j], plane[:].indirect(entries(0, NV)))
-            s0 = NV
-            for n in (S - NV,) if j < 3 else LAST_GATHERS:
-                nc.scalar.activation(values[:, s0 : s0 + n, j], rounded[:].indirect(entries(s0, s0 + n)), COPY)
+            s0 = 0
+            for g, n in enumerate(SHARES):
+                if g == 0:
+                    nc.vector.tensor_copy(picked[g][:, :, j], plane[:].indirect(entries(s0, s0 + n)))
+                else:
+                    nc.scalar.activation(picked[g][:, :, j], rounded[:].indirect(entries(s0, s0 + n)), COPY)
                 s0 += n
 
-        w_pack = keep.tile([P, N, 4], BF16, name="w_pack", align_bytes=64)
-        nc.vector.tensor_copy(w_pack[:], w_raw[:].rearrange("p j n -> p n j"))
+        w_pack = turns.tile([P, N, 4], BF16, name="w_pack", tag="codes", align_bytes=64)
+        nc.gpsimd.tensor_scalar(w_pack[:], w_raw[:].rearrange("p j n -> p n j"), 1.0, 0.0, MULT, ADD)
         w_codes = keep.tile([P, N], U32, name="w_codes", align_bytes=64)
         w_scales = keep.tile([P, N], U8, name="w_scales", align_bytes=64)
-        x_codes = keep.tile([P, S], U32, name="x_codes", align_bytes=64)
+        nc.vector.quantize_mx(
+            out=w_codes[:].bitcast(FP8X4),
+            scales=w_scales[:],
+            in_=w_pack[:].rearrange("p n j -> p (n j)"),
+        )
+        x_codes = turns.tile([P, S], U32, name="x_codes", tag="codes", align_bytes=64)
         x_scales = keep.tile([P, S], U8, name="x_scales", align_bytes=64)
         y = turns.tile([P, S], F32, name="y", tag="late", align_bytes=64)
 
         s0 = 0
-        for i, n in enumerate(PIECES):
-            cols = slice(s0, s0 + n)
-            nc.vector.quantize_mx(
-                out=x_codes[:, cols].bitcast(FP8X4),
-                scales=x_scales[:, cols],
-                in_=picked[:, 4 * s0 : 4 * (s0 + n)],
-            )
-            if i == 0:
+        for g, share in enumerate(SHARES):
+            acc = psum.tile([P, share], F32, name=f"acc{g}", tag=f"bank{g}")
+            r0 = 0
+            for n in PIECES[g]:
+                cols = slice(s0 + r0, s0 + r0 + n)
                 nc.vector.quantize_mx(
-                    out=w_codes[:].bitcast(FP8X4),
-                    scales=w_scales[:],
-                    in_=w_pack[:].rearrange("p n j -> p (n j)"),
+                    out=x_codes[:, cols].bitcast(FP8X4),
+                    scales=x_scales[:, cols],
+                    in_=picked[g][:, r0 : r0 + n, :].rearrange("p s j -> p (s j)"),
                 )
-            acc = psum.tile([P, n], F32, name=f"acc{s0}", tag=f"bank{i}")
-            nc.tensor.matmul_mx(
-                out=acc[:],
-                lhsT=w_codes[:].bitcast(FP8X4),
-                lhsT_scale=w_scales[:],
-                rhs=x_codes[:, cols].bitcast(FP8X4),
-                rhs_scale=x_scales[:, cols],
-                start=True,
-                stop=True,
-            )
-            nc.scalar.activation(y[:, cols], acc[:], SILU, bias=b_t[:])
-            s0 += n
+                nc.tensor.matmul_mx(
+                    out=acc[:, r0 : r0 + n],
+                    lhsT=w_codes[:].bitcast(FP8X4),
+                    lhsT_scale=w_scales[:],
+                    rhs=x_codes[:, cols].bitcast(FP8X4),
+                    rhs_scale=x_scales[:, cols],
+                    start=True,
+                    stop=True,
+                )
+                r0 += n
+            nc.scalar.activation(y[:, s0 : s0 + share], acc[:], SILU, bias=b_t[:])
+            s0 += share
 
         terms = [keep.tile([P, V], F32, name=f"term{d}") for d in range(D)]
         total = keep.tile([P, V], F32, name="total")

@@ -20,8 +20,9 @@ ADD = mybir.AluOpType.add
 
 CHUNKS = (1024, 512, 512)
 LAST_CHUNKS = (1024, 512, 256, 256)
-SHARES = (384, 384, 256)
-PIECES = ((256, 128), (256, 128), (256,))
+SHARES = (320, 448, 256)
+QUANT_PIECES = ((256, 64), (64, 128, 256), (256,))
+BANKS = ((256, 256), (256,), (256,))
 
 
 def tile_picked_sub_lin_silu_sub_e_kernel(
@@ -101,16 +102,22 @@ def tile_picked_sub_lin_silu_sub_e_kernel(
         y = turns.tile([P, S], F32, name="y", tag="late", align_bytes=64)
 
         s0 = 0
-        for g, share in enumerate(SHARES):
-            acc = psum.tile([P, share], F32, name=f"acc{g}", tag=f"bank{g}")
+        for g, widths in enumerate(QUANT_PIECES):
             r0 = 0
-            for n in PIECES[g]:
-                cols = slice(s0 + r0, s0 + r0 + n)
+            for n in widths:
                 nc.vector.quantize_mx(
-                    out=x_codes[:, cols].bitcast(FP8X4),
-                    scales=x_scales[:, cols],
+                    out=x_codes[:, s0 : s0 + n].bitcast(FP8X4),
+                    scales=x_scales[:, s0 : s0 + n],
                     in_=picked[g][:, r0 : r0 + n, :].rearrange("p s j -> p (s j)"),
                 )
+                r0 += n
+                s0 += n
+        s0 = 0
+        for g, widths in enumerate(BANKS):
+            acc = psum.tile([P, sum(widths)], F32, name=f"acc{g}", tag=f"bank{g}")
+            r0 = 0
+            for n in widths:
+                cols = slice(s0 + r0, s0 + r0 + n)
                 nc.tensor.matmul_mx(
                     out=acc[:, r0 : r0 + n],
                     lhsT=w_codes[:].bitcast(FP8X4),
@@ -121,8 +128,8 @@ def tile_picked_sub_lin_silu_sub_e_kernel(
                     stop=True,
                 )
                 r0 += n
-            nc.scalar.activation(y[:, s0 : s0 + share], acc[:], SILU, bias=b_t[:])
-            s0 += share
+            nc.scalar.activation(y[:, s0 : s0 + r0], acc[:], SILU, bias=b_t[:])
+            s0 += r0
 
         terms = [keep.tile([P, V], F32, name=f"term{d}") for d in range(D)]
         total = keep.tile([P, V], F32, name="total")

@@ -18,10 +18,11 @@ SILU = mybir.ActivationFunctionType.Silu
 MULT = mybir.AluOpType.mult
 ADD = mybir.AluOpType.add
 
-CHUNKS = (1024, 512, 512)
-LAST_CHUNKS = (1024, 512, 256, 256)
-SHARES = (320, 448, 256)
-QUANT_PIECES = ((256, 64), (64, 128, 256), (256,))
+FINE_CHUNKS = (1024, 512, 256, 256)
+COARSE_CHUNKS = (1024, 512, 512)
+CHUNKS = (FINE_CHUNKS, COARSE_CHUNKS, COARSE_CHUNKS, FINE_CHUNKS)
+NV = 352
+PIECE = 256
 BANKS = ((256, 256), (256,), (256,))
 
 
@@ -48,7 +49,7 @@ def tile_picked_sub_lin_silu_sub_e_kernel(
         for j in range(4):
             plane = keep.tile([P, T], F32, name=f"plane{j}", align_bytes=64)
             t0 = 0
-            for n in CHUNKS if j < 3 else LAST_CHUNKS:
+            for n in CHUNKS[j]:
                 nc.sync.dma_start(plane[:, t0 : t0 + n], x_rows[:, j, t0 : t0 + n])
                 if j == 0 and t0 == 0:
                     nc.sync.dma_start(offs_t[:], offs)
@@ -66,7 +67,7 @@ def tile_picked_sub_lin_silu_sub_e_kernel(
             nc.sync.dma_start(pos_t[:], pos)
             pos_ts.append(pos_t)
 
-        picked = [keep.tile([P, n, 4], BF16, name=f"picked{g}", align_bytes=64) for g, n in enumerate(SHARES)]
+        picked = keep.tile([P, S, 4], BF16, name="picked", align_bytes=64)
 
         def entries(s0, s1):
             return offs_t[:, s0 // 16 : s1 // 16]
@@ -77,16 +78,13 @@ def tile_picked_sub_lin_silu_sub_e_kernel(
             else:
                 rounded = turns.tile([P, T], BF16, name=f"rounded{j}", tag="late", align_bytes=64)
             t0 = 0
-            for n in CHUNKS if j < 3 else LAST_CHUNKS:
+            for n in CHUNKS[j]:
                 nc.vector.tensor_copy(rounded[:, t0 : t0 + n], plane[:, t0 : t0 + n])
                 t0 += n
-            s0 = 0
-            for g, n in enumerate(SHARES):
-                if g == 0:
-                    nc.vector.tensor_copy(picked[g][:, :, j], plane[:].indirect(entries(s0, s0 + n)))
-                else:
-                    nc.scalar.activation(picked[g][:, :, j], rounded[:].indirect(entries(s0, s0 + n)), COPY)
-                s0 += n
+            nc.vector.tensor_copy(picked[:, 0:NV, j], plane[:].indirect(entries(0, NV)))
+            cuts = (NV, S) if j < 3 else (NV, S - PIECE, S)
+            for s0, s1 in zip(cuts, cuts[1:]):
+                nc.scalar.activation(picked[:, s0:s1, j], rounded[:].indirect(entries(s0, s1)), COPY)
 
         w_pack = turns.tile([P, N, 4], BF16, name="w_pack", tag="codes", align_bytes=64)
         nc.gpsimd.tensor_scalar(w_pack[:], w_raw[:].rearrange("p j n -> p n j"), 1.0, 0.0, MULT, ADD)
@@ -101,17 +99,12 @@ def tile_picked_sub_lin_silu_sub_e_kernel(
         x_scales = keep.tile([P, S], U8, name="x_scales", align_bytes=64)
         y = turns.tile([P, S], F32, name="y", tag="late", align_bytes=64)
 
-        s0 = 0
-        for g, widths in enumerate(QUANT_PIECES):
-            r0 = 0
-            for n in widths:
-                nc.vector.quantize_mx(
-                    out=x_codes[:, s0 : s0 + n].bitcast(FP8X4),
-                    scales=x_scales[:, s0 : s0 + n],
-                    in_=picked[g][:, r0 : r0 + n, :].rearrange("p s j -> p (s j)"),
-                )
-                r0 += n
-                s0 += n
+        for s0 in range(0, S, PIECE):
+            nc.vector.quantize_mx(
+                out=x_codes[:, s0 : s0 + PIECE].bitcast(FP8X4),
+                scales=x_scales[:, s0 : s0 + PIECE],
+                in_=picked[:, s0 : s0 + PIECE, :].rearrange("p s j -> p (s j)"),
+            )
         s0 = 0
         for g, widths in enumerate(BANKS):
             acc = psum.tile([P, sum(widths)], F32, name=f"acc{g}", tag=f"bank{g}")

@@ -20,10 +20,10 @@ ADD = mybir.AluOpType.add
 
 FINE_CHUNKS = (1024, 512, 256, 256)
 COARSE_CHUNKS = (1024, 512, 512)
-CHUNKS = (FINE_CHUNKS, COARSE_CHUNKS, COARSE_CHUNKS, FINE_CHUNKS)
-NV = 352
+CHUNKS = (COARSE_CHUNKS, COARSE_CHUNKS, COARSE_CHUNKS, FINE_CHUNKS)
+NV = 384
 PIECE = 256
-BANKS = ((256, 256), (256,), (256,))
+BANKS = ((256, 128), (128, 256), (256,))
 
 
 def tile_picked_sub_lin_silu_sub_e_kernel(
@@ -59,13 +59,16 @@ def tile_picked_sub_lin_silu_sub_e_kernel(
         nc.sync.dma_start(w_raw[:], w.rearrange("(p j) n -> p j n", j=4))
         b_t = keep.tile([P, 1], F32, name="b_t")
         nc.sync.dma_start(b_t[:], b)
-        gate_t = keep.tile([P, D, V], F32, name="gate_t")
-        nc.sync.dma_start(gate_t[:], gate.rearrange("d p v -> p d v"))
         pos_ts = []
         for d, pos in enumerate((pos1, pos2, pos3, pos4)):
             pos_t = keep.tile([P, V // 16], U16, name=f"pos_t{d}")
             nc.sync.dma_start(pos_t[:], pos)
             pos_ts.append(pos_t)
+        gate_ts = []
+        for d in range(0, D, 2):
+            gate_t = keep.tile([P, 2, V], F32, name=f"gate_t{d}")
+            nc.sync.dma_start(gate_t[:], gate[d : d + 2].rearrange("d p v -> p d v"))
+            gate_ts.extend((gate_t[:, 0, :], gate_t[:, 1, :]))
 
         picked = keep.tile([P, S, 4], BF16, name="picked", align_bytes=64)
 
@@ -130,7 +133,7 @@ def tile_picked_sub_lin_silu_sub_e_kernel(
 
         def neighbour(d, v0, v1):
             nc.vector.tensor_tensor(
-                terms[d][:, v0:v1], y[:].indirect(pos_ts[d][:, v0 // 16 : v1 // 16]), gate_t[:, d, v0:v1], MULT
+                terms[d][:, v0:v1], y[:].indirect(pos_ts[d][:, v0 // 16 : v1 // 16]), gate_ts[d][:, v0:v1], MULT
             )
             if d < D - 1:
                 for c in range(v0 // P, v1 // P):

@@ -21,9 +21,10 @@ ADD = mybir.AluOpType.add
 FINE_CHUNKS = (1024, 512, 256, 256)
 COARSE_CHUNKS = (1024, 512, 512)
 CHUNKS = (COARSE_CHUNKS, COARSE_CHUNKS, COARSE_CHUNKS, FINE_CHUNKS)
-NV = 384
+VECTOR_SHARES = (352, 352, 384, 384)
 PIECE = 256
-BANKS = ((256, 128), (128, 256), (256,))
+QUANT_PIECES = (256, 256, 256, 128, 128)
+BANKS = ((256, 128), (128, 256), (128,), (128,))
 
 
 def tile_picked_sub_lin_silu_sub_e_kernel(
@@ -84,8 +85,9 @@ def tile_picked_sub_lin_silu_sub_e_kernel(
             for n in CHUNKS[j]:
                 nc.vector.tensor_copy(rounded[:, t0 : t0 + n], plane[:, t0 : t0 + n])
                 t0 += n
-            nc.vector.tensor_copy(picked[:, 0:NV, j], plane[:].indirect(entries(0, NV)))
-            cuts = (NV, S) if j < 3 else (NV, S - PIECE, S)
+            share = VECTOR_SHARES[j]
+            nc.vector.tensor_copy(picked[:, 0:share, j], plane[:].indirect(entries(0, share)))
+            cuts = (share, S) if j < 3 else (share, S - PIECE, S)
             for s0, s1 in zip(cuts, cuts[1:]):
                 nc.scalar.activation(picked[:, s0:s1, j], rounded[:].indirect(entries(s0, s1)), COPY)
 
@@ -102,12 +104,14 @@ def tile_picked_sub_lin_silu_sub_e_kernel(
         x_scales = keep.tile([P, S], U8, name="x_scales", align_bytes=64)
         y = turns.tile([P, S], F32, name="y", tag="late", align_bytes=64)
 
-        for s0 in range(0, S, PIECE):
+        s0 = 0
+        for n in QUANT_PIECES:
             nc.vector.quantize_mx(
-                out=x_codes[:, s0 : s0 + PIECE].bitcast(FP8X4),
-                scales=x_scales[:, s0 : s0 + PIECE],
-                in_=picked[:, s0 : s0 + PIECE, :].rearrange("p s j -> p (s j)"),
+                out=x_codes[:, s0 : s0 + n].bitcast(FP8X4),
+                scales=x_scales[:, s0 : s0 + n],
+                in_=picked[:, s0 : s0 + n, :].rearrange("p s j -> p (s j)"),
             )
+            s0 += n
         s0 = 0
         for g, widths in enumerate(BANKS):
             acc = psum.tile([P, sum(widths)], F32, name=f"acc{g}", tag=f"bank{g}")

@@ -23,8 +23,7 @@ COARSE_CHUNKS = (1024, 512, 512)
 CHUNKS = (COARSE_CHUNKS, COARSE_CHUNKS, COARSE_CHUNKS, FINE_CHUNKS)
 VECTOR_SHARES = (352, 352, 384, 384)
 PIECE = 256
-QUANT_PIECES = (256, 256, 256, 128, 128)
-BANKS = ((256, 128), (128, 256), (128,), (128,))
+PIECES = (256, 256, 256, 128, 128)
 
 
 def tile_picked_sub_lin_silu_sub_e_kernel(
@@ -95,41 +94,44 @@ def tile_picked_sub_lin_silu_sub_e_kernel(
         nc.gpsimd.tensor_scalar(w_pack[:], w_raw[:].rearrange("p j n -> p n j"), 1.0, 0.0, MULT, ADD)
         w_codes = keep.tile([P, N], U32, name="w_codes", align_bytes=64)
         w_scales = keep.tile([P, N], U8, name="w_scales", align_bytes=64)
+        x_scales = keep.tile([P, S], U8, name="x_scales", align_bytes=64)
+        y = turns.tile([P, S], F32, name="y", tag="late", align_bytes=64)
+
+        def quantise(codes, s0, n):
+            nc.vector.quantize_mx(
+                out=codes.bitcast(FP8X4),
+                scales=x_scales[:, s0 : s0 + n],
+                in_=picked[:, s0 : s0 + n, :].rearrange("p s j -> p (s j)"),
+            )
+
+        first = PIECES[0]
+        first_codes = keep.tile([P, first], U32, name="first_codes", align_bytes=64)
+        quantise(first_codes[:], 0, first)
         nc.vector.quantize_mx(
             out=w_codes[:].bitcast(FP8X4),
             scales=w_scales[:],
             in_=w_pack[:].rearrange("p n j -> p (n j)"),
         )
-        x_codes = turns.tile([P, S], U32, name="x_codes", tag="codes", align_bytes=64)
-        x_scales = keep.tile([P, S], U8, name="x_scales", align_bytes=64)
-        y = turns.tile([P, S], F32, name="y", tag="late", align_bytes=64)
-
+        later_codes = turns.tile([P, S - first], U32, name="later_codes", tag="codes", align_bytes=64)
         s0 = 0
-        for n in QUANT_PIECES:
-            nc.vector.quantize_mx(
-                out=x_codes[:, s0 : s0 + n].bitcast(FP8X4),
-                scales=x_scales[:, s0 : s0 + n],
-                in_=picked[:, s0 : s0 + n, :].rearrange("p s j -> p (s j)"),
+        for i, n in enumerate(PIECES):
+            if i == 0:
+                codes = first_codes[:]
+            else:
+                codes = later_codes[:, s0 - first : s0 - first + n]
+                quantise(codes, s0, n)
+            acc = psum.tile([P, n], F32, name=f"acc{i}", tag=f"bank{i}")
+            nc.tensor.matmul_mx(
+                out=acc[:],
+                lhsT=w_codes[:].bitcast(FP8X4),
+                lhsT_scale=w_scales[:],
+                rhs=codes.bitcast(FP8X4),
+                rhs_scale=x_scales[:, s0 : s0 + n],
+                start=True,
+                stop=True,
             )
+            nc.scalar.activation(y[:, s0 : s0 + n], acc[:], SILU, bias=b_t[:])
             s0 += n
-        s0 = 0
-        for g, widths in enumerate(BANKS):
-            acc = psum.tile([P, sum(widths)], F32, name=f"acc{g}", tag=f"bank{g}")
-            r0 = 0
-            for n in widths:
-                cols = slice(s0 + r0, s0 + r0 + n)
-                nc.tensor.matmul_mx(
-                    out=acc[:, r0 : r0 + n],
-                    lhsT=w_codes[:].bitcast(FP8X4),
-                    lhsT_scale=w_scales[:],
-                    rhs=x_codes[:, cols].bitcast(FP8X4),
-                    rhs_scale=x_scales[:, cols],
-                    start=True,
-                    stop=True,
-                )
-                r0 += n
-            nc.scalar.activation(y[:, s0 : s0 + r0], acc[:], SILU, bias=b_t[:])
-            s0 += r0
 
         terms = [keep.tile([P, V], F32, name=f"term{d}") for d in range(D)]
         total = keep.tile([P, V], F32, name="total")

@@ -21,9 +21,11 @@ ADD = mybir.AluOpType.add
 FINE_CHUNKS = (1024, 512, 256, 256)
 COARSE_CHUNKS = (1024, 512, 512)
 CHUNKS = (COARSE_CHUNKS, COARSE_CHUNKS, COARSE_CHUNKS, FINE_CHUNKS)
+LOAD_ORDER = (2, 0, 1, 3)
 VECTOR_SHARES = (352, 352, 384, 384)
 PIECE = 256
 PIECES = (256, 256, 256, 128, 128)
+THIRD_SPANS = ((0, 256), (256, 384), (384, 512))
 
 
 def tile_picked_sub_lin_silu_sub_e_kernel(
@@ -45,16 +47,16 @@ def tile_picked_sub_lin_silu_sub_e_kernel(
 
         x_rows = xT.rearrange("(p j) t -> p j t", j=4)
         offs_t = keep.tile([P, S // 16], U16, name="offs_t")
-        planes = []
-        for j in range(4):
+        planes = {}
+        for j in LOAD_ORDER:
             plane = keep.tile([P, T], F32, name=f"plane{j}", align_bytes=64)
             t0 = 0
             for n in CHUNKS[j]:
                 nc.sync.dma_start(plane[:, t0 : t0 + n], x_rows[:, j, t0 : t0 + n])
-                if j == 0 and t0 == 0:
+                if j == LOAD_ORDER[0] and t0 == 0:
                     nc.sync.dma_start(offs_t[:], offs)
                 t0 += n
-            planes.append(plane)
+            planes[j] = plane
         w_raw = keep.tile([P, 4, N], F32, name="w_raw")
         nc.sync.dma_start(w_raw[:], w.rearrange("(p j) n -> p j n", j=4))
         b_t = keep.tile([P, 1], F32, name="b_t")
@@ -75,7 +77,8 @@ def tile_picked_sub_lin_silu_sub_e_kernel(
         def entries(s0, s1):
             return offs_t[:, s0 // 16 : s1 // 16]
 
-        for j, plane in enumerate(planes):
+        for j in LOAD_ORDER:
+            plane = planes[j]
             if j < 3:
                 rounded = keep.tile([P, T], BF16, name=f"rounded{j}", align_bytes=64)
             else:
@@ -91,7 +94,7 @@ def tile_picked_sub_lin_silu_sub_e_kernel(
                 nc.scalar.activation(picked[:, s0:s1, j], rounded[:].indirect(entries(s0, s1)), COPY)
 
         w_pack = turns.tile([P, N, 4], BF16, name="w_pack", tag="codes", align_bytes=64)
-        nc.gpsimd.tensor_scalar(w_pack[:], w_raw[:].rearrange("p j n -> p n j"), 1.0, 0.0, MULT, ADD)
+        nc.gpsimd.tensor_scalar(w_pack[:], w_raw[:].rearrange("p j n -> p n j"), 1.0, warmed[:], MULT, ADD)
         w_codes = keep.tile([P, N], U32, name="w_codes", align_bytes=64)
         w_scales = keep.tile([P, N], U8, name="w_scales", align_bytes=64)
         x_scales = keep.tile([P, S], U8, name="x_scales", align_bytes=64)
@@ -154,16 +157,13 @@ def tile_picked_sub_lin_silu_sub_e_kernel(
 
         neighbour(0, 0, V)
         neighbour(1, 0, V)
-        backs = []
-        for h in range(2):
-            neighbour(2, h * V // 2, (h + 1) * V // 2)
-            back = psum.tile([P, V // 2], F32, name=f"back{h}", tag=f"bank{h}")
-            for i in range(2):
-                c = 2 * h + i
+        backs = [psum.tile([P, V // 2], F32, name=f"back{h}", tag=f"bank{h}") for h in range(2)]
+        for v0, v1 in THIRD_SPANS:
+            neighbour(2, v0, v1)
+            for c in range(v0 // P, v1 // P):
                 sum_t = keep.tile([P, P], F32, name=f"sum_t{c}")
                 nc.scalar.copy(sum_t[:], turned[c][:])
-                nc.tensor.transpose(back[:, i * P : (i + 1) * P], sum_t[:], ident[:])
-            backs.append(back)
+                nc.tensor.transpose(backs[c // 2][:, c % 2 * P : (c % 2 + 1) * P], sum_t[:], ident[:])
         for h in range(2):
             neighbour(3, h * V // 2, (h + 1) * V // 2)
         for h in range(2):

@@ -157,16 +157,16 @@ def tile_picked_sub_lin_silu_sub_e_kernel(
 
         neighbour(0, 0, V)
         neighbour(1, 0, V)
-        backs = [psum.tile([P, V // 2], F32, name=f"back{h}", tag=f"bank{h}") for h in range(2)]
-        for v0, v1 in THIRD_SPANS:
+        backs = [psum.tile([P, v1 - v0], F32, name=f"back{i}", tag=f"bank{i}") for i, (v0, v1) in enumerate(THIRD_SPANS)]
+        for i, (v0, v1) in enumerate(THIRD_SPANS):
             neighbour(2, v0, v1)
             for c in range(v0 // P, v1 // P):
                 sum_t = keep.tile([P, P], F32, name=f"sum_t{c}")
                 nc.scalar.copy(sum_t[:], turned[c][:])
-                nc.tensor.transpose(backs[c // 2][:, c % 2 * P : (c % 2 + 1) * P], sum_t[:], ident[:])
+                nc.tensor.transpose(backs[i][:, c * P - v0 : (c + 1) * P - v0], sum_t[:], ident[:])
         for h in range(2):
             neighbour(3, h * V // 2, (h + 1) * V // 2)
-        for h in range(2):
-            half = slice(h * V // 2, (h + 1) * V // 2)
-            nc.vector.tensor_add(total[:, half], backs[h][:], terms[D - 1][:, half])
-            nc.sync.dma_start(out[:, half], total[:, half])
+        for i, (v0, v1) in enumerate(THIRD_SPANS):
+            nc.vector.tensor_add(total[:, v0:v1], backs[i][:], terms[D - 1][:, v0:v1])
+            if v1 % (V // 2) == 0:
+                nc.sync.dma_start(out[:, v1 - V // 2 : v1], total[:, v1 - V // 2 : v1])

@@ -22,7 +22,7 @@ FINE_CHUNKS = (1024, 512, 256, 256)
 COARSE_CHUNKS = (1024, 512, 512)
 CHUNKS = (COARSE_CHUNKS, COARSE_CHUNKS, COARSE_CHUNKS, FINE_CHUNKS)
 LOAD_ORDER = (2, 0, 1, 3)
-VECTOR_SHARES = (352, 352, 384, 384)
+VECTOR_SHARES = (352, 352, 384, 352)
 PIECE = 256
 PIECES = (256, 256, 256, 128, 128)
 THIRD_SPANS = ((0, 256), (256, 384), (384, 512))

@@ -57,7 +57,7 @@ def tile_picked_sub_lin_silu_sub_e_kernel(
                     nc.sync.dma_start(offs_t[:], offs)
                 t0 += n
             planes[j] = plane
-        w_raw = keep.tile([P, 4, N], F32, name="w_raw")
+        w_raw = turns.tile([P, 4, N], F32, name="w_raw", tag="codes", align_bytes=64)
         nc.sync.dma_start(w_raw[:], w.rearrange("(p j) n -> p j n", j=4))
         b_t = keep.tile([P, 1], F32, name="b_t")
         nc.sync.dma_start(b_t[:], b)
@@ -79,10 +79,7 @@ def tile_picked_sub_lin_silu_sub_e_kernel(
 
         for j in LOAD_ORDER:
             plane = planes[j]
-            if j < 3:
-                rounded = keep.tile([P, T], BF16, name=f"rounded{j}", align_bytes=64)
-            else:
-                rounded = turns.tile([P, T], BF16, name=f"rounded{j}", tag="late", align_bytes=64)
+            rounded = keep.tile([P, T], BF16, name=f"rounded{j}", align_bytes=64)
             t0 = 0
             for n in CHUNKS[j]:
                 nc.vector.tensor_copy(rounded[:, t0 : t0 + n], plane[:, t0 : t0 + n])
@@ -93,12 +90,12 @@ def tile_picked_sub_lin_silu_sub_e_kernel(
             for s0, s1 in zip(cuts, cuts[1:]):
                 nc.scalar.activation(picked[:, s0:s1, j], rounded[:].indirect(entries(s0, s1)), COPY)
 
-        w_pack = turns.tile([P, N, 4], BF16, name="w_pack", tag="codes", align_bytes=64)
+        w_pack = keep.tile([P, N, 4], BF16, name="w_pack", align_bytes=64)
         nc.gpsimd.tensor_scalar(w_pack[:], w_raw[:].rearrange("p j n -> p n j"), 1.0, warmed[:], MULT, ADD)
         w_codes = keep.tile([P, N], U32, name="w_codes", align_bytes=64)
         w_scales = keep.tile([P, N], U8, name="w_scales", align_bytes=64)
         x_scales = keep.tile([P, S], U8, name="x_scales", align_bytes=64)
-        y = turns.tile([P, S], F32, name="y", tag="late", align_bytes=64)
+        y = keep.tile([P, S], F32, name="y", align_bytes=64)
 
         def quantise(codes, s0, n):
             nc.vector.quantize_mx(

@@ -20,12 +20,12 @@ ADD = mybir.AluOpType.add
 
 FINE_CHUNKS = (1024, 512, 256, 256)
 COARSE_CHUNKS = (1024, 512, 512)
-CHUNKS = (COARSE_CHUNKS, COARSE_CHUNKS, COARSE_CHUNKS, FINE_CHUNKS)
+CHUNKS = (COARSE_CHUNKS, COARSE_CHUNKS, (1280, 768), FINE_CHUNKS)
 LOAD_ORDER = (2, 0, 1, 3)
 VECTOR_SHARES = (352, 352, 384, 352)
 PIECE = 256
 PIECES = (256, 256, 256, 128, 128)
-THIRD_SPANS = ((0, 256), (256, 384), (384, 512))
+HALF = V // 2
 
 
 def tile_picked_sub_lin_silu_sub_e_kernel(
@@ -45,6 +45,9 @@ def tile_picked_sub_lin_silu_sub_e_kernel(
         ident = keep.tile([P, P], F32, name="ident")
         make_identity(nc, ident[:])
 
+        gate_rows = keep.tile([P, HALF], F32, name="gate_rows")
+        nc.gpsimd.memset(gate_rows[:], 0.0)
+
         x_rows = xT.rearrange("(p j) t -> p j t", j=4)
         offs_t = keep.tile([P, S // 16], U16, name="offs_t")
         planes = {}
@@ -55,6 +58,8 @@ def tile_picked_sub_lin_silu_sub_e_kernel(
                 nc.sync.dma_start(plane[:, t0 : t0 + n], x_rows[:, j, t0 : t0 + n])
                 if j == LOAD_ORDER[0] and t0 == 0:
                     nc.sync.dma_start(offs_t[:], offs)
+                if j == LOAD_ORDER[0] and t0 == CHUNKS[j][0]:
+                    nc.sync.dma_start(gate_rows[0 : D - 1, :], gate[1:D, 0, 0:HALF])
                 t0 += n
             planes[j] = plane
         w_raw = turns.tile([P, 4, N], F32, name="w_raw", tag="codes", align_bytes=64)
@@ -66,11 +71,16 @@ def tile_picked_sub_lin_silu_sub_e_kernel(
             pos_t = keep.tile([P, V // 16], U16, name=f"pos_t{d}")
             nc.sync.dma_start(pos_t[:], pos)
             pos_ts.append(pos_t)
-        gate_ts = []
-        for d in range(0, D, 2):
-            gate_t = keep.tile([P, 2, V], F32, name=f"gate_t{d}")
-            nc.sync.dma_start(gate_t[:], gate[d : d + 2].rearrange("d p v -> p d v"))
-            gate_ts.extend((gate_t[:, 0, :], gate_t[:, 1, :]))
+        gate_late = keep.tile([P, D - 1, HALF], F32, name="gate_late")
+        nc.sync.dma_start(gate_late[:], gate[1:D, :, HALF:V].rearrange("d p v -> p d v"))
+        gate_first = keep.tile([P, V], F32, name="gate_first")
+        nc.sync.dma_start(gate_first[:], gate[0])
+
+        gate_turned = psum.tile([P, HALF], F32, name="gate_turned", tag="bank5")
+        for c in range(2):
+            nc.tensor.transpose(gate_turned[:, c * P : (c + 1) * P], gate_rows[:, c * P : (c + 1) * P], ident[:])
+        gate_cols = keep.tile([P, 2, D - 1], F32, name="gate_cols")
+        nc.vector.tensor_copy(gate_cols[:], gate_turned[:].rearrange("p (c d) -> p c d", c=2)[:, :, 0 : D - 1])
 
         picked = keep.tile([P, S, 4], BF16, name="picked", align_bytes=64)
 
@@ -133,37 +143,60 @@ def tile_picked_sub_lin_silu_sub_e_kernel(
             nc.scalar.activation(y[:, s0 : s0 + n], acc[:], SILU, bias=b_t[:])
             s0 += n
 
-        terms = [keep.tile([P, V], F32, name=f"term{d}") for d in range(D)]
         total = keep.tile([P, V], F32, name="total")
-        turned = [psum.tile([P, P], F32, name=f"turned{c}", tag=f"bank{4 + c}") for c in range(V // P)]
-
-        def neighbour(d, v0, v1):
+        first_term = keep.tile([P, V], F32, name="first_term")
+        plain_turned = []
+        terms = []
+        sum_turned = psum.tile([P, P], F32, name="sum_turned", tag="bank0")
+        for d in range(1, D):
+            plain = keep.tile([P, HALF], F32, name=f"plain{d}")
+            nc.scalar.activation(plain[:], y[:].indirect(pos_ts[d][:, 0 : HALF // 16]), COPY)
+            turned = psum.tile([P, HALF], F32, name=f"plain_turned{d}", tag=f"bank{4 + d}")
+            for c in range(2):
+                nc.tensor.transpose(turned[:, c * P : (c + 1) * P], plain[:, c * P : (c + 1) * P], ident[:])
+            plain_turned.append(turned)
+            term = keep.tile([P, HALF], F32, name=f"term{d}")
             nc.vector.tensor_tensor(
-                terms[d][:, v0:v1], y[:].indirect(pos_ts[d][:, v0 // 16 : v1 // 16]), gate_ts[d][:, v0:v1], MULT
+                term[:], y[:].indirect(pos_ts[d][:, HALF // 16 : V // 16]), gate_late[:, d - 1, :], MULT
             )
-            if d < D - 1:
-                for c in range(v0 // P, v1 // P):
-                    nc.tensor.matmul(
-                        turned[c][:],
-                        terms[d][:, c * P : (c + 1) * P],
-                        ident[:],
-                        start=(d == 0),
-                        stop=(d == D - 2),
-                        is_transpose=True,
-                    )
+            terms.append(term)
+            nc.tensor.matmul(
+                sum_turned[:], term[:, 0:P], ident[:], start=(d == 1), stop=(d == D - 1), is_transpose=True
+            )
 
-        neighbour(0, 0, V)
-        neighbour(1, 0, V)
-        backs = [psum.tile([P, v1 - v0], F32, name=f"back{i}", tag=f"bank{i}") for i, (v0, v1) in enumerate(THIRD_SPANS)]
-        for i, (v0, v1) in enumerate(THIRD_SPANS):
-            neighbour(2, v0, v1)
-            for c in range(v0 // P, v1 // P):
-                sum_t = keep.tile([P, P], F32, name=f"sum_t{c}")
-                nc.scalar.copy(sum_t[:], turned[c][:])
-                nc.tensor.transpose(backs[i][:, c * P - v0 : (c + 1) * P - v0], sum_t[:], ident[:])
-        for h in range(2):
-            neighbour(3, h * V // 2, (h + 1) * V // 2)
-        for i, (v0, v1) in enumerate(THIRD_SPANS):
-            nc.vector.tensor_add(total[:, v0:v1], backs[i][:], terms[D - 1][:, v0:v1])
-            if v1 % (V // 2) == 0:
-                nc.sync.dma_start(out[:, v1 - V // 2 : v1], total[:, v1 - V // 2 : v1])
+        def first(v0, v1):
+            nc.vector.tensor_tensor(
+                first_term[:, v0:v1], y[:].indirect(pos_ts[0][:, v0 // 16 : v1 // 16]), gate_first[:, v0:v1], MULT
+            )
+
+        two = keep.tile([P, P], F32, name="two")
+        three = keep.tile([P, P], F32, name="three")
+        nc.vector.tensor_add(two[:], terms[0][:, P:HALF], terms[1][:, P:HALF])
+        first(HALF, V)
+        nc.vector.tensor_add(three[:], two[:], terms[2][:, P:HALF])
+        first(0, HALF)
+        nc.vector.tensor_add(total[:, V - P : V], three[:], first_term[:, V - P : V])
+
+        backs = [psum.tile([P, P], F32, name=f"back{c}", tag=f"bank{1 + c}") for c in range(3)]
+
+        def weigh(d):
+            for c in range(2):
+                weighted = keep.tile([P, P], F32, name=f"weighted{d}_{c}")
+                nc.scalar.activation(
+                    weighted[:], plain_turned[d - 1][:, c * P : (c + 1) * P], COPY, scale=gate_cols[:, c, d - 1 : d]
+                )
+                nc.tensor.matmul(
+                    backs[c][:], weighted[:], ident[:], start=(d == 1), stop=(d == D - 1), is_transpose=True
+                )
+
+        weigh(1)
+        weigh(2)
+        sum_t = keep.tile([P, P], F32, name="sum_t")
+        nc.scalar.copy(sum_t[:], sum_turned[:])
+        nc.tensor.transpose(backs[2][:], sum_t[:], ident[:])
+        weigh(3)
+        for c in (2, 0, 1):
+            nc.vector.tensor_add(total[:, c * P : (c + 1) * P], backs[c][:], first_term[:, c * P : (c + 1) * P])
+            if c > 0:
+                v0 = c // 2 * HALF
+                nc.sync.dma_start(out[:, v0 : v0 + HALF], total[:, v0 : v0 + HALF])

@@ -144,59 +144,36 @@ def tile_picked_sub_lin_silu_sub_e_kernel(
             s0 += n
 
         total = keep.tile([P, V], F32, name="total")
-        first_term = keep.tile([P, V], F32, name="first_term")
-        plain_turned = []
-        terms = []
-        sum_turned = psum.tile([P, P], F32, name="sum_turned", tag="bank0")
+
+        def gated(dst, d, v0, v1, weights):
+            nc.vector.tensor_tensor(dst, y[:].indirect(pos_ts[d][:, v0 // 16 : v1 // 16]), weights, MULT)
+
+        turned = {}
+        for c in range(2):
+            for d in range(1, D):
+                plain = keep.tile([P, P], F32, name=f"plain{d}_{c}")
+                nc.scalar.activation(plain[:], y[:].indirect(pos_ts[d][:, c * P // 16 : (c + 1) * P // 16]), COPY)
+                turned[c, d] = psum.tile([P, P], F32, name=f"turned{d}_{c}", tag=f"bank{2 + 3 * c + d - 1}")
+                nc.tensor.transpose(turned[c, d][:], plain[:], ident[:])
+
+        terms = [keep.tile([P, HALF], F32, name=f"term{d}") for d in range(D)]
+        two = keep.tile([P, HALF], F32, name="two")
+        three = keep.tile([P, HALF], F32, name="three")
+        first_term = keep.tile([P, HALF], F32, name="first_term")
         for d in range(1, D):
-            plain = keep.tile([P, HALF], F32, name=f"plain{d}")
-            nc.scalar.activation(plain[:], y[:].indirect(pos_ts[d][:, 0 : HALF // 16]), COPY)
-            turned = psum.tile([P, HALF], F32, name=f"plain_turned{d}", tag=f"bank{4 + d}")
-            for c in range(2):
-                nc.tensor.transpose(turned[:, c * P : (c + 1) * P], plain[:, c * P : (c + 1) * P], ident[:])
-            plain_turned.append(turned)
-            term = keep.tile([P, HALF], F32, name=f"term{d}")
-            nc.vector.tensor_tensor(
-                term[:], y[:].indirect(pos_ts[d][:, HALF // 16 : V // 16]), gate_late[:, d - 1, :], MULT
-            )
-            terms.append(term)
-            nc.tensor.matmul(
-                sum_turned[:], term[:, 0:P], ident[:], start=(d == 1), stop=(d == D - 1), is_transpose=True
-            )
+            gated(terms[d][:], d, HALF, V, gate_late[:, d - 1, :])
+        nc.vector.tensor_add(two[:], terms[1][:], terms[2][:])
+        gated(terms[0][:], 0, HALF, V, gate_first[:, HALF:V])
+        nc.vector.tensor_add(three[:], two[:], terms[3][:])
+        gated(first_term[:], 0, 0, HALF, gate_first[:, 0:HALF])
+        nc.vector.tensor_add(total[:, HALF:V], three[:], terms[0][:])
+        nc.sync.dma_start(out[:, HALF:V], total[:, HALF:V])
 
-        def first(v0, v1):
-            nc.vector.tensor_tensor(
-                first_term[:, v0:v1], y[:].indirect(pos_ts[0][:, v0 // 16 : v1 // 16]), gate_first[:, v0:v1], MULT
-            )
-
-        two = keep.tile([P, P], F32, name="two")
-        three = keep.tile([P, P], F32, name="three")
-        nc.vector.tensor_add(two[:], terms[0][:, P:HALF], terms[1][:, P:HALF])
-        first(HALF, V)
-        nc.vector.tensor_add(three[:], two[:], terms[2][:, P:HALF])
-        first(0, HALF)
-        nc.vector.tensor_add(total[:, V - P : V], three[:], first_term[:, V - P : V])
-
-        backs = [psum.tile([P, P], F32, name=f"back{c}", tag=f"bank{1 + c}") for c in range(3)]
-
-        def weigh(d):
-            for c in range(2):
+        for c in range(2):
+            back = psum.tile([P, P], F32, name=f"back{c}", tag=f"bank{c}")
+            for d in range(1, D):
                 weighted = keep.tile([P, P], F32, name=f"weighted{d}_{c}")
-                nc.scalar.activation(
-                    weighted[:], plain_turned[d - 1][:, c * P : (c + 1) * P], COPY, scale=gate_cols[:, c, d - 1 : d]
-                )
-                nc.tensor.matmul(
-                    backs[c][:], weighted[:], ident[:], start=(d == 1), stop=(d == D - 1), is_transpose=True
-                )
-
-        weigh(1)
-        weigh(2)
-        sum_t = keep.tile([P, P], F32, name="sum_t")
-        nc.scalar.copy(sum_t[:], sum_turned[:])
-        nc.tensor.transpose(backs[2][:], sum_t[:], ident[:])
-        weigh(3)
-        for c in (2, 0, 1):
-            nc.vector.tensor_add(total[:, c * P : (c + 1) * P], backs[c][:], first_term[:, c * P : (c + 1) * P])
-            if c > 0:
-                v0 = c // 2 * HALF
-                nc.sync.dma_start(out[:, v0 : v0 + HALF], total[:, v0 : v0 + HALF])
+                nc.scalar.activation(weighted[:], turned[c, d][:], COPY, scale=gate_cols[:, c, d - 1 : d])
+                nc.tensor.matmul(back[:], weighted[:], ident[:], start=(d == 1), stop=(d == D - 1), is_transpose=True)
+            nc.vector.tensor_add(total[:, c * P : (c + 1) * P], back[:], first_term[:, c * P : (c + 1) * P])
+        nc.sync.dma_start(out[:, 0:HALF], total[:, 0:HALF])

@@ -18,12 +18,11 @@ SILU = mybir.ActivationFunctionType.Silu
 MULT = mybir.AluOpType.mult
 ADD = mybir.AluOpType.add
 
-FINE_CHUNKS = (1024, 512, 256, 256)
-COARSE_CHUNKS = (1024, 512, 512)
-CHUNKS = (COARSE_CHUNKS, COARSE_CHUNKS, (1280, 768), FINE_CHUNKS)
-LOAD_ORDER = (2, 0, 1, 3)
-VECTOR_SHARES = (352, 352, 384, 352)
-PIECE = 256
+LAST_CHUNKS = (1024, 512, 256, 256)
+SHARE = 352
+WOVEN_END = 480
+EARLY_SPANS = ((SHARE, 704), (704, S))
+LATER_SPANS = ((WOVEN_END, 768), (768, S))
 PIECES = (256, 256, 256, 128, 128)
 HALF = V // 2
 
@@ -50,18 +49,18 @@ def tile_picked_sub_lin_silu_sub_e_kernel(
 
         x_rows = xT.rearrange("(p j) t -> p j t", j=4)
         offs_t = keep.tile([P, S // 16], U16, name="offs_t")
-        planes = {}
-        for j in LOAD_ORDER:
+        planes = []
+        for j in range(4):
             plane = keep.tile([P, T], F32, name=f"plane{j}", align_bytes=64)
             t0 = 0
-            for n in CHUNKS[j]:
+            for n in LAST_CHUNKS if j == 3 else (T,):
                 nc.sync.dma_start(plane[:, t0 : t0 + n], x_rows[:, j, t0 : t0 + n])
-                if j == LOAD_ORDER[0] and t0 == 0:
-                    nc.sync.dma_start(offs_t[:], offs)
-                if j == LOAD_ORDER[0] and t0 == CHUNKS[j][0]:
-                    nc.sync.dma_start(gate_rows[0 : D - 1, :], gate[1:D, 0, 0:HALF])
                 t0 += n
-            planes[j] = plane
+            if j == 0:
+                nc.sync.dma_start(offs_t[:], offs)
+                for d in range(1, D):
+                    nc.sync.dma_start(gate_rows[d - 1 : d, :], gate[d, 0:1, 0:HALF])
+            planes.append(plane)
         w_raw = turns.tile([P, 4, N], F32, name="w_raw", tag="codes", align_bytes=64)
         nc.sync.dma_start(w_raw[:], w.rearrange("(p j) n -> p j n", j=4))
         b_t = keep.tile([P, 1], F32, name="b_t")
@@ -74,7 +73,8 @@ def tile_picked_sub_lin_silu_sub_e_kernel(
         gate_late = keep.tile([P, D - 1, HALF], F32, name="gate_late")
         nc.sync.dma_start(gate_late[:], gate[1:D, :, HALF:V].rearrange("d p v -> p d v"))
         gate_first = keep.tile([P, V], F32, name="gate_first")
-        nc.sync.dma_start(gate_first[:], gate[0])
+        for v0 in (HALF, 0):
+            nc.sync.dma_start(gate_first[:, v0 : v0 + HALF], gate[0, :, v0 : v0 + HALF])
 
         gate_turned = psum.tile([P, HALF], F32, name="gate_turned", tag="bank5")
         for c in range(2):
@@ -87,18 +87,34 @@ def tile_picked_sub_lin_silu_sub_e_kernel(
         def entries(s0, s1):
             return offs_t[:, s0 // 16 : s1 // 16]
 
-        for j in LOAD_ORDER:
-            plane = planes[j]
-            rounded = keep.tile([P, T], BF16, name=f"rounded{j}", align_bytes=64)
-            t0 = 0
-            for n in CHUNKS[j]:
-                nc.vector.tensor_copy(rounded[:, t0 : t0 + n], plane[:, t0 : t0 + n])
-                t0 += n
-            share = VECTOR_SHARES[j]
-            nc.vector.tensor_copy(picked[:, 0:share, j], plane[:].indirect(entries(0, share)))
-            cuts = (share, S) if j < 3 else (share, S - PIECE, S)
-            for s0, s1 in zip(cuts, cuts[1:]):
-                nc.scalar.activation(picked[:, s0:s1, j], rounded[:].indirect(entries(s0, s1)), COPY)
+        def direct(j):
+            nc.vector.tensor_copy(picked[:, 0:SHARE, j], planes[j][:].indirect(entries(0, SHARE)))
+
+        def fetch(dst, j, s0, s1):
+            nc.scalar.activation(dst, planes[j][:].indirect(entries(s0, s1)), COPY)
+
+        for j in range(3):
+            direct(j)
+            for s0, s1 in EARLY_SPANS if j < 2 else LATER_SPANS:
+                fetched = keep.tile([P, s1 - s0], BF16, name=f"fetched{j}_{s0}", align_bytes=64)
+                fetch(fetched[:], j, s0, s1)
+                nc.vector.tensor_copy(picked[:, s0:s1, j], fetched[:])
+        late = keep.tile([P, 2, WOVEN_END - SHARE], BF16, name="late", align_bytes=64)
+        fetch(late[:, 0, :], 2, SHARE, WOVEN_END)
+
+        rounded = keep.tile([P, T], BF16, name="rounded", align_bytes=64)
+        t0 = 0
+        for i, n in enumerate(LAST_CHUNKS):
+            if i == 0:
+                nc.scalar.copy(rounded[:, t0 : t0 + n], planes[3][:, t0 : t0 + n])
+            else:
+                nc.vector.tensor_copy(rounded[:, t0 : t0 + n], planes[3][:, t0 : t0 + n])
+            t0 += n
+        direct(3)
+        fetch(late[:, 1, :], 3, SHARE, WOVEN_END)
+        for s0, s1 in LATER_SPANS:
+            nc.scalar.activation(picked[:, s0:s1, 3], rounded[:].indirect(entries(s0, s1)), COPY)
+        nc.vector.tensor_copy(picked[:, SHARE:WOVEN_END, 2:4], late[:].rearrange("p j s -> p s j"))
 
         w_pack = keep.tile([P, N, 4], BF16, name="w_pack", align_bytes=64)
         nc.gpsimd.tensor_scalar(w_pack[:], w_raw[:].rearrange("p j n -> p n j"), 1.0, warmed[:], MULT, ADD)
@@ -165,9 +181,10 @@ def tile_picked_sub_lin_silu_sub_e_kernel(
         nc.vector.tensor_add(two[:], terms[1][:], terms[2][:])
         gated(terms[0][:], 0, HALF, V, gate_first[:, HALF:V])
         nc.vector.tensor_add(three[:], two[:], terms[3][:])
-        gated(first_term[:], 0, 0, HALF, gate_first[:, 0:HALF])
+        gated(first_term[:, 0:P], 0, 0, P, gate_first[:, 0:P])
         nc.vector.tensor_add(total[:, HALF:V], three[:], terms[0][:])
         nc.sync.dma_start(out[:, HALF:V], total[:, HALF:V])
+        gated(first_term[:, P:HALF], 0, P, HALF, gate_first[:, P:HALF])
 
         for c in range(2):
             back = psum.tile([P, P], F32, name=f"back{c}", tag=f"bank{c}")
@@ -176,4 +193,4 @@ def tile_picked_sub_lin_silu_sub_e_kernel(
                 nc.scalar.activation(weighted[:], turned[c, d][:], COPY, scale=gate_cols[:, c, d - 1 : d])
                 nc.tensor.matmul(back[:], weighted[:], ident[:], start=(d == 1), stop=(d == D - 1), is_transpose=True)
             nc.vector.tensor_add(total[:, c * P : (c + 1) * P], back[:], first_term[:, c * P : (c + 1) * P])
-        nc.sync.dma_start(out[:, 0:HALF], total[:, 0:HALF])
+            nc.sync.dma_start(out[:, c * P : (c + 1) * P], total[:, c * P : (c + 1) * P])

@@ -19,10 +19,11 @@ MULT = mybir.AluOpType.mult
 ADD = mybir.AluOpType.add
 
 LAST_CHUNKS = (1024, 512, 256, 256)
-SHARE = 352
+SHARES = (352, 352, 352, 352)
 WOVEN_END = 480
-EARLY_SPANS = ((SHARE, 704), (704, S))
-LATER_SPANS = ((WOVEN_END, 768), (768, S))
+EARLY_SPANS = ((SHARES[0], 704), (704, S))
+LAST_SPANS = ((WOVEN_END, 768), (768, S))
+SPANS = (EARLY_SPANS, EARLY_SPANS, LAST_SPANS)
 PIECES = (256, 256, 256, 128, 128)
 HALF = V // 2
 
@@ -58,11 +59,10 @@ def tile_picked_sub_lin_silu_sub_e_kernel(
                 t0 += n
             if j == 0:
                 nc.sync.dma_start(offs_t[:], offs)
-                for d in range(1, D):
-                    nc.sync.dma_start(gate_rows[d - 1 : d, :], gate[d, 0:1, 0:HALF])
             planes.append(plane)
         w_raw = turns.tile([P, 4, N], F32, name="w_raw", tag="codes", align_bytes=64)
         nc.sync.dma_start(w_raw[:], w.rearrange("(p j) n -> p j n", j=4))
+        nc.sync.dma_start(gate_rows[0 : D - 1, :], gate[1:D, 0, 0:HALF])
         b_t = keep.tile([P, 1], F32, name="b_t")
         nc.sync.dma_start(b_t[:], b)
         pos_ts = []
@@ -79,8 +79,6 @@ def tile_picked_sub_lin_silu_sub_e_kernel(
         gate_turned = psum.tile([P, HALF], F32, name="gate_turned", tag="bank5")
         for c in range(2):
             nc.tensor.transpose(gate_turned[:, c * P : (c + 1) * P], gate_rows[:, c * P : (c + 1) * P], ident[:])
-        gate_cols = keep.tile([P, 2, D - 1], F32, name="gate_cols")
-        nc.vector.tensor_copy(gate_cols[:], gate_turned[:].rearrange("p (c d) -> p c d", c=2)[:, :, 0 : D - 1])
 
         picked = keep.tile([P, S, 4], BF16, name="picked", align_bytes=64)
 
@@ -88,19 +86,19 @@ def tile_picked_sub_lin_silu_sub_e_kernel(
             return offs_t[:, s0 // 16 : s1 // 16]
 
         def direct(j):
-            nc.vector.tensor_copy(picked[:, 0:SHARE, j], planes[j][:].indirect(entries(0, SHARE)))
+            nc.vector.tensor_copy(picked[:, 0 : SHARES[j], j], planes[j][:].indirect(entries(0, SHARES[j])))
 
         def fetch(dst, j, s0, s1):
             nc.scalar.activation(dst, planes[j][:].indirect(entries(s0, s1)), COPY)
 
         for j in range(3):
             direct(j)
-            for s0, s1 in EARLY_SPANS if j < 2 else LATER_SPANS:
+            for s0, s1 in SPANS[j]:
                 fetched = keep.tile([P, s1 - s0], BF16, name=f"fetched{j}_{s0}", align_bytes=64)
                 fetch(fetched[:], j, s0, s1)
                 nc.vector.tensor_copy(picked[:, s0:s1, j], fetched[:])
-        late = keep.tile([P, 2, WOVEN_END - SHARE], BF16, name="late", align_bytes=64)
-        fetch(late[:, 0, :], 2, SHARE, WOVEN_END)
+        late = keep.tile([P, 2, WOVEN_END - SHARES[3]], BF16, name="late", align_bytes=64)
+        fetch(late[:, 0, :], 2, SHARES[3], WOVEN_END)
 
         rounded = keep.tile([P, T], BF16, name="rounded", align_bytes=64)
         t0 = 0
@@ -111,10 +109,10 @@ def tile_picked_sub_lin_silu_sub_e_kernel(
                 nc.vector.tensor_copy(rounded[:, t0 : t0 + n], planes[3][:, t0 : t0 + n])
             t0 += n
         direct(3)
-        fetch(late[:, 1, :], 3, SHARE, WOVEN_END)
-        for s0, s1 in LATER_SPANS:
+        fetch(late[:, 1, :], 3, SHARES[3], WOVEN_END)
+        for s0, s1 in LAST_SPANS:
             nc.scalar.activation(picked[:, s0:s1, 3], rounded[:].indirect(entries(s0, s1)), COPY)
-        nc.vector.tensor_copy(picked[:, SHARE:WOVEN_END, 2:4], late[:].rearrange("p j s -> p s j"))
+        nc.vector.tensor_copy(picked[:, SHARES[3] : WOVEN_END, 2:4], late[:].rearrange("p j s -> p s j"))
 
         w_pack = keep.tile([P, N, 4], BF16, name="w_pack", align_bytes=64)
         nc.gpsimd.tensor_scalar(w_pack[:], w_raw[:].rearrange("p j n -> p n j"), 1.0, warmed[:], MULT, ADD)
@@ -158,6 +156,9 @@ def tile_picked_sub_lin_silu_sub_e_kernel(
             )
             nc.scalar.activation(y[:, s0 : s0 + n], acc[:], SILU, bias=b_t[:])
             s0 += n
+
+        gate_cols = turns.tile([P, 2, D - 1], F32, name="gate_cols", tag="codes", align_bytes=64)
+        nc.vector.tensor_copy(gate_cols[:], gate_turned[:].rearrange("p (c d) -> p c d", c=2)[:, :, 0 : D - 1])
 
         total = keep.tile([P, V], F32, name="total")
 

from contextlib import ExitStack

import concourse.mybir as mybir
from concourse.masks import make_identity

K, T, D, S, V, N = 512, 2048, 4, 1024, 512, 128
P = 128
FLOPS = 2 * K * N * S

F32 = mybir.dt.float32
BF16 = mybir.dt.bfloat16
U32 = mybir.dt.uint32
U16 = mybir.dt.uint16
U8 = mybir.dt.uint8
FP8X4 = mybir.dt.float8_e4m3fn_x4
COPY = mybir.ActivationFunctionType.Copy
SILU = mybir.ActivationFunctionType.Silu
MULT = mybir.AluOpType.mult
ADD = mybir.AluOpType.add

LAST_CHUNKS = (1024, 512, 256, 256)
SHARES = (352, 352, 352, 352)
WOVEN_END = 480
EARLY_SPANS = ((SHARES[0], 704), (704, S))
LAST_SPANS = ((WOVEN_END, 768), (768, S))
SPANS = (EARLY_SPANS, EARLY_SPANS, LAST_SPANS)
PIECES = (256, 256, 256, 128, 128)
HALF = V // 2


def tile_picked_sub_lin_silu_sub_e_kernel(
    tc, xT, w, b, gate, offs, pos1, pos2, pos3, pos4, out
):
    nc = tc.nc
    with ExitStack() as ctx:
        keep = ctx.enter_context(tc.tile_pool(name="keep", bufs=1))
        turns = ctx.enter_context(tc.tile_pool(name="turns", bufs=1))
        psum = ctx.enter_context(tc.psum_pool(name="psum", bufs=1))

        warm = keep.tile([P, 1], F32, name="warm")
        warmed = keep.tile([P, 1], F32, name="warmed")
        nc.gpsimd.memset(warm[:], 0.0)
        nc.scalar.activation(warmed[:], warm[:], SILU)

        ident = keep.tile([P, P], F32, name="ident")
        make_identity(nc, ident[:])

        gate_rows = keep.tile([P, HALF], F32, name="gate_rows")
        nc.gpsimd.memset(gate_rows[:], 0.0)

        x_rows = xT.rearrange("(p j) t -> p j t", j=4)
        offs_t = keep.tile([P, S // 16], U16, name="offs_t")
        planes = []
        for j in range(4):
            plane = keep.tile([P, T], F32, name=f"plane{j}", align_bytes=64)
            t0 = 0
            for n in LAST_CHUNKS if j == 3 else (T,):
                nc.sync.dma_start(plane[:, t0 : t0 + n], x_rows[:, j, t0 : t0 + n])
                t0 += n
            if j == 0:
                nc.sync.dma_start(offs_t[:], offs)
            planes.append(plane)
        w_raw = turns.tile([P, 4, N], F32, name="w_raw", tag="codes", align_bytes=64)
        nc.sync.dma_start(w_raw[:], w.rearrange("(p j) n -> p j n", j=4))
        nc.sync.dma_start(gate_rows[0 : D - 1, :], gate[1:D, 0, 0:HALF])
        b_t = keep.tile([P, 1], F32, name="b_t")
        nc.sync.dma_start(b_t[:], b)
        pos_ts = []
        for d, pos in enumerate((pos1, pos2, pos3, pos4)):
            pos_t = keep.tile([P, V // 16], U16, name=f"pos_t{d}")
            nc.sync.dma_start(pos_t[:], pos)
            pos_ts.append(pos_t)
        gate_late = keep.tile([P, D - 1, HALF], F32, name="gate_late")
        nc.sync.dma_start(gate_late[:], gate[1:D, :, HALF:V].rearrange("d p v -> p d v"))
        gate_first = keep.tile([P, V], F32, name="gate_first")
        for v0 in (HALF, 0):
            nc.sync.dma_start(gate_first[:, v0 : v0 + HALF], gate[0, :, v0 : v0 + HALF])

        gate_turned = psum.tile([P, HALF], F32, name="gate_turned", tag="bank5")
        for c in range(2):
            nc.tensor.transpose(gate_turned[:, c * P : (c + 1) * P], gate_rows[:, c * P : (c + 1) * P], ident[:])

        picked = keep.tile([P, S, 4], BF16, name="picked", align_bytes=64)

        def entries(s0, s1):
            return offs_t[:, s0 // 16 : s1 // 16]

        def direct(j):
            nc.vector.tensor_copy(picked[:, 0 : SHARES[j], j], planes[j][:].indirect(entries(0, SHARES[j])))

        def fetch(dst, j, s0, s1):
            nc.scalar.activation(dst, planes[j][:].indirect(entries(s0, s1)), COPY)

        for j in range(3):
            direct(j)
            for s0, s1 in SPANS[j]:
                fetched = keep.tile([P, s1 - s0], BF16, name=f"fetched{j}_{s0}", align_bytes=64)
                fetch(fetched[:], j, s0, s1)
                nc.vector.tensor_copy(picked[:, s0:s1, j], fetched[:])
        late = keep.tile([P, 2, WOVEN_END - SHARES[3]], BF16, name="late", align_bytes=64)
        fetch(late[:, 0, :], 2, SHARES[3], WOVEN_END)

        rounded = keep.tile([P, T], BF16, name="rounded", align_bytes=64)
        t0 = 0
        for i, n in enumerate(LAST_CHUNKS):
            if i == 0:
                nc.scalar.copy(rounded[:, t0 : t0 + n], planes[3][:, t0 : t0 + n])
            else:
                nc.vector.tensor_copy(rounded[:, t0 : t0 + n], planes[3][:, t0 : t0 + n])
            t0 += n
        direct(3)
        fetch(late[:, 1, :], 3, SHARES[3], WOVEN_END)
        for s0, s1 in LAST_SPANS:
            nc.scalar.activation(picked[:, s0:s1, 3], rounded[:].indirect(entries(s0, s1)), COPY)
        nc.vector.tensor_copy(picked[:, SHARES[3] : WOVEN_END, 2:4], late[:].rearrange("p j s -> p s j"))

        w_pack = keep.tile([P, N, 4], BF16, name="w_pack", align_bytes=64)
        nc.gpsimd.tensor_scalar(w_pack[:], w_raw[:].rearrange("p j n -> p n j"), 1.0, warmed[:], MULT, ADD)
        w_codes = keep.tile([P, N], U32, name="w_codes", align_bytes=64)
        w_scales = keep.tile([P, N], U8, name="w_scales", align_bytes=64)
        x_scales = keep.tile([P, S], U8, name="x_scales", align_bytes=64)
        y = keep.tile([P, S], F32, name="y", align_bytes=64)

        def quantise(codes, s0, n):
            nc.vector.quantize_mx(
                out=codes.bitcast(FP8X4),
                scales=x_scales[:, s0 : s0 + n],
                in_=picked[:, s0 : s0 + n, :].rearrange("p s j -> p (s j)"),
            )

        first = PIECES[0]
        first_codes = keep.tile([P, first], U32, name="first_codes", align_bytes=64)
        quantise(first_codes[:], 0, first)
        nc.vector.quantize_mx(
            out=w_codes[:].bitcast(FP8X4),
            scales=w_scales[:],
            in_=w_pack[:].rearrange("p n j -> p (n j)"),
        )
        later_codes = turns.tile([P, S - first], U32, name="later_codes", tag="codes", align_bytes=64)
        s0 = 0
        for i, n in enumerate(PIECES):
            if i == 0:
                codes = first_codes[:]
            else:
                codes = later_codes[:, s0 - first : s0 - first + n]
                quantise(codes, s0, n)
            acc = psum.tile([P, n], F32, name=f"acc{i}", tag=f"bank{i}")
            nc.tensor.matmul_mx(
                out=acc[:],
                lhsT=w_codes[:].bitcast(FP8X4),
                lhsT_scale=w_scales[:],
                rhs=codes.bitcast(FP8X4),
                rhs_scale=x_scales[:, s0 : s0 + n],
                start=True,
                stop=True,
            )
            nc.scalar.activation(y[:, s0 : s0 + n], acc[:], SILU, bias=b_t[:])
            s0 += n

        gate_cols = turns.tile([P, 2, D - 1], F32, name="gate_cols", tag="codes", align_bytes=64)
        nc.vector.tensor_copy(gate_cols[:], gate_turned[:].rearrange("p (c d) -> p c d", c=2)[:, :, 0 : D - 1])

        total = keep.tile([P, V], F32, name="total")

        def gated(dst, d, v0, v1, weights):
            nc.vector.tensor_tensor(dst, y[:].indirect(pos_ts[d][:, v0 // 16 : v1 // 16]), weights, MULT)

        turned = {}
        for c in range(2):
            for d in range(1, D):
                plain = keep.tile([P, P], F32, name=f"plain{d}_{c}")
                nc.scalar.activation(plain[:], y[:].indirect(pos_ts[d][:, c * P // 16 : (c + 1) * P // 16]), COPY)
                turned[c, d] = psum.tile([P, P], F32, name=f"turned{d}_{c}", tag=f"bank{2 + 3 * c + d - 1}")
                nc.tensor.transpose(turned[c, d][:], plain[:], ident[:])

        terms = [keep.tile([P, HALF], F32, name=f"term{d}") for d in range(D)]
        two = keep.tile([P, HALF], F32, name="two")
        three = keep.tile([P, HALF], F32, name="three")
        first_term = keep.tile([P, HALF], F32, name="first_term")
        for d in range(1, D):
            gated(terms[d][:], d, HALF, V, gate_late[:, d - 1, :])
        nc.vector.tensor_add(two[:], terms[1][:], terms[2][:])
        gated(terms[0][:], 0, HALF, V, gate_first[:, HALF:V])
        nc.vector.tensor_add(three[:], two[:], terms[3][:])
        gated(first_term[:, 0:P], 0, 0, P, gate_first[:, 0:P])
        nc.vector.tensor_add(total[:, HALF:V], three[:], terms[0][:])
        nc.sync.dma_start(out[:, HALF:V], total[:, HALF:V])
        gated(first_term[:, P:HALF], 0, P, HALF, gate_first[:, P:HALF])

        for c in range(2):
            back = psum.tile([P, P], F32, name=f"back{c}", tag=f"bank{c}")
            for d in range(1, D):
                weighted = keep.tile([P, P], F32, name=f"weighted{d}_{c}")
                nc.scalar.activation(weighted[:], turned[c, d][:], COPY, scale=gate_cols[:, c, d - 1 : d])
                nc.tensor.matmul(back[:], weighted[:], ident[:], start=(d == 1), stop=(d == D - 1), is_transpose=True)
            nc.vector.tensor_add(total[:, c * P : (c + 1) * P], back[:], first_term[:, c * P : (c + 1) * P])
            nc.sync.dma_start(out[:, c * P : (c + 1) * P], total[:, c * P : (c + 1) * P])
